import numpy as np
import ml_dtypes


def mxq(x, axis, fmt="e4m3"):
    dtype, down = {"e4m3": (ml_dtypes.float8_e4m3fn, 7), "e5m2": (ml_dtypes.float8_e5m2, 14)}[fmt]
    v = np.moveaxis(np.asarray(x, np.float32).astype(ml_dtypes.bfloat16).astype(np.float64), axis, -1)
    blocks = v.reshape(v.shape[:-1] + (-1, 32))
    amax = np.abs(blocks).max(-1, keepdims=True)
    byte = np.maximum(np.where(amax > 0, np.frexp(amax)[1] - 1 + 127, 0) - down, 1)
    scale = np.exp2(byte - 127.0)
    codes = (blocks / scale).astype(np.float32).astype(dtype).astype(np.float64)
    return np.moveaxis((codes * scale).reshape(v.shape), -1, axis)


WIDE = False


def mx_kscale(k):
    if not WIDE:
        return np.ones(k)
    levels = np.array([10, -10, 5, -5, 0])
    if k % 512:
        return np.exp2(np.random.permutation(np.resize(levels, k // 32))).repeat(32)
    a = np.empty((k // 512, 16))
    for p in range(k // 512):
        a[p, :8] = np.random.permutation(np.resize(levels, 8))
        for g in range(8):
            far = levels[np.abs(levels - a[p, g]) >= 10]
            a[p, g + 8] = far[np.random.randint(len(far))]
    return np.exp2(a.ravel()).repeat(32)


def f64(x):
    return np.asarray(x).astype(np.float64)


def striped(idx):
    return np.tile(idx.reshape(-1, 16).T, (8, 1)).astype(np.uint16)


def unstriped(offs):
    return offs[:16].T.reshape(-1).astype(np.int64)


E2M1 = np.array([0.0, 0.5, 1.0, 1.5, 2.0, 3.0, 4.0, 6.0, -0.0, -0.5, -1.0, -1.5, -2.0, -3.0, -4.0, -6.0])


def pack_weight(w, fmt):
    k, n = w.shape
    w = f64(np.asarray(w, np.float32).astype(ml_dtypes.bfloat16)).reshape(k // 32, 32, n)
    amax = np.abs(w).max(1)
    if fmt == "e4m3":
        byte = np.frexp(amax)[1] - 1 + 127 - 7
    else:
        mant, ex = np.frexp(amax / 6.0)
        byte = np.where(mant > 0.5, ex, ex - 1) + 127
    byte = np.clip(np.where(amax > 0, byte, 1), 1, 254)
    scaled = (w * np.exp2(127.0 - byte)[:, None, :]).reshape(k, n).astype(np.float32)
    by_word = np.ascontiguousarray(scaled.reshape(k // 512, 128, 4, n).transpose(0, 1, 3, 2))
    if fmt == "e4m3":
        words = by_word.astype(ml_dtypes.float8_e4m3fn).view(np.uint8)
    else:
        c = by_word.astype(ml_dtypes.float4_e2m1fn).view(np.uint8) & 0xF
        words = (c[..., 0::2] | (c[..., 1::2] << 4)).reshape(k // 512, 128, 2 * n)
    return np.ascontiguousarray(words), np.ascontiguousarray(byte.astype(np.uint8).reshape(k // 512, 16, n))


def unpack_weight(words, scales, fmt):
    g, _, n = scales.shape
    words = np.ascontiguousarray(words).reshape(g, 128, n, -1)
    if fmt == "e4m3":
        vals = words.view(ml_dtypes.float8_e4m3fn).astype(np.float64)
    else:
        nib = np.empty((g, 128, n, 4), np.uint8)
        nib[..., 0::2] = words & 0xF
        nib[..., 1::2] = words >> 4
        vals = E2M1[nib]
    vals = vals * np.repeat(np.exp2(scales.astype(np.float64) - 127.0), 8, axis=1)[..., None]
    return vals.transpose(0, 1, 3, 2).reshape(g * 512, n)


def gelu(v):
    return 0.5 * v * (1.0 + np.tanh(np.sqrt(2.0 / np.pi) * (v + 0.044715 * v**3)))


def striped8(idx):
    return np.concatenate([v.reshape(-1, 16).T for v in idx]).astype(np.uint16)


def unstriped8(offs):
    return np.stack([offs[16 * g:16 * g + 16].T.reshape(-1) for g in range(8)]).astype(np.int64)


def runs(v, idx8):
    k = np.arange(v.shape[0])
    return v[k[:, None], idx8[k % 512 // 64]]


K, T, S, P, H, N = 1024, 2048, 1024, 512, 1536, 384


def setup_inputs():
    n = np.random.standard_normal
    s = mx_kscale(K)[:, None]
    u = mx_kscale(H)[:, None]
    d = {}
    d["tab_words"], d["tab_scales"] = pack_weight(n((K, T)) * s, "e4m3")
    d["offs"] = striped8(np.stack([np.random.permutation(T)[:S] for _ in range(8)]))
    d["pos1"] = striped(np.random.permutation(S)[:P])
    d["pos2"] = striped(np.random.permutation(S)[:P])
    d["w1"] = (n((K, H)) / K ** 0.5 / s).astype(np.float32)
    d["swing"] = np.random.uniform(1.4, 2.9, H).astype(np.float32)
    d["amp_out"] = (np.exp(0.3 * n(H)) * u[:, 0]).astype(np.float32)
    d["amp_home"] = (np.exp(0.3 * n(H)) * u[:, 0]).astype(np.float32)
    d["w2_words"], d["w2_scales"] = pack_weight(n((H, N)) / H ** 0.5 / u, "e2m1")
    return d


def reference(tab_words, tab_scales, offs, pos1, pos2, w1, swing, amp_out, amp_home, w2_words, w2_scales):
    v = runs(unpack_weight(tab_words, tab_scales, "e4m3"), unstriped8(offs))
    h = f64(swing)[:, None] * np.tanh(mxq(f64(w1), 0, "e4m3").T @ v)
    xo = f64(amp_out)[:, None] * np.sin(h[:, unstriped(pos1)])
    xh = f64(amp_home)[:, None] * np.cos(h[:, unstriped(pos2)])
    w2 = unpack_weight(w2_words, w2_scales, "e2m1")
    yo = w2.T @ mxq(xo, 0, "e4m3")
    yh = w2.T @ mxq(xh, 0, "e4m3")
    return np.maximum(yo, yh)

@@ -1,0 +1,268 @@
+import math
+from contextlib import ExitStack
+
+import concourse.mybir as mybir
+
+K, T, S, M, H, N = 1024, 2048, 1024, 512, 1536, 384
+FLOPS = 2 * K * H * S + 2 * 2 * H * N * M
+
+F32 = mybir.dt.float32
+BF16 = mybir.dt.bfloat16
+I32 = mybir.dt.int32
+U32 = mybir.dt.uint32
+U16 = mybir.dt.uint16
+U8 = mybir.dt.uint8
+FP8X4 = mybir.dt.float8_e4m3fn_x4
+FP4X4 = mybir.dt.float4_e2m1fn_x4
+ACT = mybir.ActivationFunctionType
+ALU = mybir.AluOpType
+
+P = 128
+PACK = 4
+KP = P * PACK
+A = K // KP
+B = H // KP
+C = N // P
+BANK = 512
+
+
+def tile_list_pigeon_bearing_support_kernel(
+    tc, tab_words, tab_scales, offs, pos1, pos2, w1, swing, amp_out, amp_home, w2_words, w2_scales, out
+):
+    nc = tc.nc
+    with ExitStack() as ctx:
+        held = ctx.enter_context(tc.tile_pool(name="held", bufs=1))
+        ring = ctx.enter_context(tc.tile_pool(name="ring", bufs=2))
+        psum = ctx.enter_context(tc.psum_pool(name="psum", bufs=1))
+
+        offs_t = held.tile([P, S // 16], U16, name="offs_t")
+        pos1_t = held.tile([P, M // 16], U16, name="pos1_t")
+        pos2_t = held.tile([P, M // 16], U16, name="pos2_t")
+        tabs = held.tile([P, T], U8, name="tabs", align_bytes=64)
+        vw = [held.tile([P, S], U32, name=f"vw{a}", align_bytes=64) for a in range(A)]
+        vs_raw = held.tile([P, S], U8, name="vs_raw", tag="vs_raw", align_bytes=64)
+        vs = held.tile([P, S], U8, name="vs", align_bytes=64)
+        w2s = held.tile([P, B, N], U8, name="w2s", align_bytes=64)
+        swing_t = held.tile([P, B, PACK], F32, name="swing_t")
+        ampo_t = held.tile([P, B, PACK], F32, name="ampo_t")
+        amph_t = held.tile([P, B, PACK], F32, name="amph_t")
+        seeds = [held.tile([P, 1], F32, name=f"seed{a}", tag=f"tabw{a}", align_bytes=64) for a in range(A)]
+        zero = held.tile([P, 1], F32, name="zero")
+        half_pi = held.tile([P, 1], F32, name="half_pi")
+
+        nc.gpsimd.memset(seeds[1][:], 0.0)
+        nc.vector.memset(tabs[:].bitcast(I32), 0)
+        nc.vector.memset(seeds[0][:], 0.0)
+        nc.gpsimd.memset(w2s[:].rearrange("p b n -> p (b n)").bitcast(I32), 0)
+        nc.scalar.activation(out=zero[:], in_=seeds[1][:], func=ACT.Silu)
+        nc.vector.tensor_scalar(half_pi[:], seeds[0][:], math.pi / 2, None, ALU.add)
+        tabw = [held.tile([P, T], I32, name=f"tabw{a}", tag=f"tabw{a}", align_bytes=64) for a in range(A)]
+
+        w1raw = {}
+
+        def load_w1(b, a):
+            rows = w1[a * KP : (a + 1) * KP, b * KP : (b + 1) * KP].rearrange("(p j) c -> p j c", j=PACK)
+            if b > 0 and a == 0:
+                raw = held.tile([P, PACK, KP], F32, name=f"w1late{b}", tag=f"tabw{b - 1}", align_bytes=64)
+                nc.sync.dma_start(raw[:], rows)
+                for half in range(2):
+                    w1raw[b, a, half] = raw[:, :, half * 256 : half * 256 + 256]
+                return
+            for half in range(2):
+                raw = ring.tile([P, PACK, 256], F32, name="w1raw")
+                nc.sync.dma_start(raw[:], rows[:, :, half * 256 : half * 256 + 256])
+                w1raw[b, a, half] = raw[:]
+
+        nc.sync.dma_start(offs_t[:], offs)
+        nc.sync.dma_start(pos1_t[:], pos1)
+        nc.sync.dma_start(pos2_t[:], pos2)
+        load_w1(0, 0)
+        for a in range(A):
+            for r in range(2):
+                nc.sync.dma_start(
+                    tabs[4 * a + r : P : 16, :].bitcast(I32), tab_scales[a, r:16:2, :].bitcast(I32)
+                )
+        for a in range(A):
+            nc.sync.dma_start(tabw[a][:], tab_words[a].rearrange("p t i -> p (t i)").bitcast(I32))
+        for vec, tile in ((swing, swing_t), (amp_out, ampo_t), (amp_home, amph_t)):
+            nc.gpsimd.dma_start(tile[:], vec.rearrange("(b p t) -> p b t", p=P, t=PACK))
+        for q in range(4):
+            nc.gpsimd.dma_start(
+                w2s[32 * q : 32 * q + 4].bitcast(I32),
+                w2_scales[:, 4 * q : 4 * q + 4, :].rearrange("b r n -> r b n").bitcast(I32),
+            )
+
+        w1g, w1c, w1s = {}, {}, {}
+
+        def weave_w1(b, a, half, engine):
+            if half == 0:
+                w1g[b, a] = ring.tile([P, PACK * KP], BF16, name="w1g", align_bytes=64)
+            ms = slice(half * 64, half * 64 + 64)
+            src = w1raw[b, a, half].rearrange("p j (m t) -> p m j t", t=PACK)
+            dst = w1g[b, a][:].rearrange("p (t m j) -> p m j t", t=PACK, j=PACK)[:, ms]
+            if engine == "S":
+                nc.scalar.copy(dst, src)
+            elif engine == "V":
+                nc.vector.tensor_copy(dst, src)
+            else:
+                nc.gpsimd.tensor_scalar(
+                    dst.rearrange("p m j t -> p m t j"), src.rearrange("p m j t -> p m t j"), 1.0, 0.0, ALU.mult, ALU.add
+                )
+
+        def quant_w1(b, a, pieces):
+            w1c[b, a] = held.tile([P, KP], U32, name=f"w1c{b}{a}", align_bytes=64)
+            w1s[b, a] = held.tile([P, KP], U8, name=f"w1s{b}{a}", align_bytes=64)
+            width = KP // pieces
+            for i in range(pieces):
+                cols = slice(i * width, (i + 1) * width)
+                nc.vector.quantize_mx(
+                    out=w1c[b, a][:, cols].bitcast(FP8X4),
+                    scales=w1s[b, a][:, cols],
+                    in_=w1g[b, a][:, PACK * i * width : PACK * (i + 1) * width],
+                )
+
+        weave_w1(0, 0, 0, "S")
+        weave_w1(0, 0, 1, "S")
+        load_w1(0, 1)
+
+        nc.vector.tensor_copy(vs_raw[:], tabs[:].indirect(offs_t[:]))
+        nc.vector.tensor_copy(vs[:].bitcast(I32), vs_raw[:].bitcast(I32))
+        for a in range(A):
+            for r in range(2):
+                nc.scalar.dma_start(
+                    vs[4 * a + 2 + r : P : 32, :].bitcast(I32), vs_raw[16 + 4 * a + r : P : 32, :].bitcast(I32)
+                )
+        nc.vector.tensor_copy(vw[0][:], tabw[0][:].bitcast(U32).indirect(offs_t[:]))
+        quant_w1(0, 0, 1)
+        nc.vector.tensor_copy(vw[1][:], tabw[1][:].bitcast(U32).indirect(offs_t[:]))
+        weave_w1(0, 1, 0, "S")
+        weave_w1(0, 1, 1, "V")
+        quant_w1(0, 1, PACK)
+        w2w = held.tile([P, B, 2 * N], U8, name="w2w", tag="vs_raw", align_bytes=64)
+        nc.sync.dma_start(w2w[:].bitcast(I32), w2_words.rearrange("b p c -> p b c").bitcast(I32))
+
+        windows = {}
+
+        def stage1(j):
+            b, t = divmod(j, PACK)
+            win = ring.tile([P, S], F32, name="win", bufs=4)
+            cols = slice(t * P, (t + 1) * P)
+            for h in range(S // BANK):
+                z = psum.tile([P, BANK], F32, name=f"z{h}")
+                hs = slice(h * BANK, (h + 1) * BANK)
+                for a in range(A):
+                    nc.tensor.matmul_mx(
+                        out=z[:],
+                        lhsT=w1c[b, a][:, cols].bitcast(FP8X4),
+                        lhsT_scale=w1s[b, a][:, cols],
+                        rhs=vw[a][:, hs].bitcast(FP8X4),
+                        rhs_scale=vs[4 * a : P, hs],
+                        start=(a == 0),
+                        stop=(a == A - 1),
+                    )
+                nc.scalar.activation(out=win[:, hs], in_=z[:], func=ACT.Tanh, bias=zero[:])
+            windows[j] = win
+
+        gh, go, so, ah = {}, {}, {}, {}
+
+        def gathers(j):
+            b, t = divmod(j, PACK)
+            if t == 0:
+                gh[b] = ring.tile([P, PACK, M], F32, name="gh")
+                go[b] = ring.tile([P, PACK, M], F32, name="go")
+            nc.vector.tensor_copy(go[b][:, t, :], windows[j][:].indirect(pos1_t[:]))
+            nc.vector.tensor_copy(gh[b][:, t, :], windows[j][:].indirect(pos2_t[:]))
+
+        def angles(j):
+            b, t = divmod(j, PACK)
+            if t == 0:
+                ah[b] = ring.tile([P, PACK, M], F32, name="ah")
+                so[b] = ring.tile([P, PACK, M], F32, name="so")
+            sw = swing_t[:, b, t : t + 1]
+            nc.scalar.activation(out=so[b][:, t, :], in_=go[b][:, t, :], func=ACT.Sin, scale=sw, bias=zero[:])
+            nc.scalar.activation(out=ah[b][:, t, :], in_=gh[b][:, t, :], func=ACT.Abs, scale=sw, bias=zero[:])
+
+        yo = [psum.tile([P, M], F32, name=f"yo{c}") for c in range(C)]
+        yh = [psum.tile([P, M], F32, name=f"yh{c}") for c in range(C)]
+
+        def stage2(b, x, y):
+            xc = ring.tile([P, M], U32, name="xc", align_bytes=64)
+            xs = ring.tile([P, M], U8, name="xs", align_bytes=64)
+            nc.vector.quantize_mx(out=xc[:].bitcast(FP8X4), scales=xs[:], in_=x[:])
+            for c in range(C):
+                nc.tensor.matmul_mx(
+                    out=y[c][:],
+                    lhsT=w2w[:, b, 2 * P * c : 2 * P * (c + 1)].bitcast(FP4X4),
+                    lhsT_scale=w2s[:, b, P * c : P * (c + 1)],
+                    rhs=xc[:].bitcast(FP8X4),
+                    rhs_scale=xs[:],
+                    start=(b == 0),
+                    stop=(b == B - 1),
+                )
+
+        def finish_home(b):
+            ch = ring.tile([P, M, PACK], F32, name="ch", bufs=1)
+            for half in range(2):
+                ms = slice(half * 256, half * 256 + 256)
+                nc.scalar.activation(
+                    out=ch[:, ms, :],
+                    in_=ah[b][:].rearrange("p t m -> p m t")[:, ms, :],
+                    func=ACT.Sin,
+                    scale=-1.0,
+                    bias=half_pi[:],
+                )
+            xh = ring.tile([P, M * PACK], BF16, name="xh", align_bytes=64)
+            xv = xh[:].rearrange("p (m t) -> p m t", t=PACK)
+            if b in ():
+                for half in range(2):
+                    ms = slice(half * 256, half * 256 + 256)
+                    nc.gpsimd.tensor_tensor(
+                        xv[:, ms, :], ch[:, ms, :], amph_t[:, b, :].unsqueeze(1).to_broadcast([P, 256, PACK]), ALU.mult
+                    )
+            else:
+                nc.vector.tensor_tensor(xv, ch[:], amph_t[:, b, :].unsqueeze(1).to_broadcast([P, M, PACK]), ALU.mult)
+            return xh
+
+        def finish_out(b):
+            xo = ring.tile([P, M * PACK], BF16, name="xo", align_bytes=64)
+            nc.vector.tensor_tensor(
+                xo[:].rearrange("p (c i t) -> p c t i", i=4, t=PACK),
+                so[b][:].rearrange("p t (c i) -> p c t i", i=4),
+                ampo_t[:, b, :].unsqueeze(1).unsqueeze(3).to_broadcast([P, M // 4, PACK, 4]),
+                ALU.mult,
+            )
+            return xo
+
+        J = B * PACK
+        LG, LA = 2, 4
+        WP = {1: [(0, 0), (0, 1)], 2: [(1, 0), (1, 1)]}
+        WE = "SSVVSSSS"
+        for step in range(J + LA):
+            if step < J:
+                stage1(step)
+                b, t = divmod(step, PACK)
+                if b + 1 < B:
+                    if t == 0:
+                        load_w1(b + 1, 0)
+                        load_w1(b + 1, 1)
+                    for a, half in WP.get(t, []):
+                        weave_w1(b + 1, a, half, WE[4 * b + 2 * a + half])
+                        if half == 1:
+                            quant_w1(b + 1, a, 1)
+            if LG <= step < J + LG:
+                gathers(step - LG)
+            if LA <= step:
+                angles(step - LA)
+                b, t = divmod(step - LA, PACK)
+                if t == PACK - 1:
+                    xo = finish_out(b)
+                    xh = finish_home(b)
+                    stage2(b, xo, yo)
+                    stage2(b, xh, yh)
+
+        for c in range(C):
+            yo_sb = ring.tile([P, M], F32, name="yo_sb", bufs=3)
+            nc.scalar.copy(yo_sb[:], yo[c][:])
+            res = ring.tile([P, M], F32, name="res", bufs=3)
+            nc.vector.tensor_tensor(res[:], yh[c][:], yo_sb[:], ALU.max)
+            nc.sync.dma_start(out[c * P : (c + 1) * P, :], res[:])

@@ -148,7 +148,7 @@ def tile_list_pigeon_bearing_support_kernel(
             win = ring.tile([P, S], F32, name="win", bufs=4)
             cols = slice(t * P, (t + 1) * P)
             for h in range(S // BANK):
-                z = psum.tile([P, BANK], F32, name=f"z{h}")
+                z = psum.tile([P, BANK], F32, name="z", tag=f"z{h}", bufs=2)
                 hs = slice(h * BANK, (h + 1) * BANK)
                 for a in range(A):
                     nc.tensor.matmul_mx(
@@ -183,22 +183,30 @@ def tile_list_pigeon_bearing_support_kernel(
             nc.scalar.activation(out=ah[b][:, t, :], in_=gh[b][:, t, :], func=ACT.Abs, scale=sw, bias=zero[:])
 
         yo = [psum.tile([P, M], F32, name=f"yo{c}") for c in range(C)]
-        yh = [psum.tile([P, M], F32, name=f"yh{c}") for c in range(C)]
+        yh = [psum.tile([P, M], F32, name="yh0")]
+        owed = []
+
+        def second_pass(b, c, xc, xs, y):
+            nc.tensor.matmul_mx(
+                out=y[c][:],
+                lhsT=w2w[:, b, 2 * P * c : 2 * P * (c + 1)].bitcast(FP4X4),
+                lhsT_scale=w2s[:, b, P * c : P * (c + 1)],
+                rhs=xc[:].bitcast(FP8X4),
+                rhs_scale=xs[:],
+                start=(b == 0),
+                stop=(b == B - 1),
+            )
 
         def stage2(b, x, y):
-            xc = ring.tile([P, M], U32, name="xc", align_bytes=64)
-            xs = ring.tile([P, M], U8, name="xs", align_bytes=64)
+            leg = "o" if y is yo else "h"
+            xc = ring.tile([P, M], U32, name="xc", tag=f"xc{leg}", align_bytes=64, bufs=B)
+            xs = ring.tile([P, M], U8, name="xs", tag=f"xs{leg}", align_bytes=64, bufs=B)
             nc.vector.quantize_mx(out=xc[:].bitcast(FP8X4), scales=xs[:], in_=x[:])
             for c in range(C):
-                nc.tensor.matmul_mx(
-                    out=y[c][:],
-                    lhsT=w2w[:, b, 2 * P * c : 2 * P * (c + 1)].bitcast(FP4X4),
-                    lhsT_scale=w2s[:, b, P * c : P * (c + 1)],
-                    rhs=xc[:].bitcast(FP8X4),
-                    rhs_scale=xs[:],
-                    start=(b == 0),
-                    stop=(b == B - 1),
-                )
+                if c < len(y):
+                    second_pass(b, c, xc, xs, y)
+                else:
+                    owed.append((b, c, xc, xs))
 
         def finish_home(b):
             ch = ring.tile([P, M, PACK], F32, name="ch", bufs=1)
@@ -213,7 +221,7 @@ def tile_list_pigeon_bearing_support_kernel(
                 )
             xh = ring.tile([P, M * PACK], BF16, name="xh", align_bytes=64)
             xv = xh[:].rearrange("p (m t) -> p m t", t=PACK)
-            if b in ():
+            if b in (0, 1):
                 for half in range(2):
                     ms = slice(half * 256, half * 256 + 256)
                     nc.gpsimd.tensor_tensor(
@@ -234,9 +242,9 @@ def tile_list_pigeon_bearing_support_kernel(
             return xo
 
         J = B * PACK
-        LG, LA = 2, 4
-        WP = {1: [(0, 0), (0, 1)], 2: [(1, 0), (1, 1)]}
-        WE = "SSVVSSSS"
+        LG, LA = 1, 3
+        WP = {0: [(0, 0)], 1: [(0, 1)], 2: [(1, 0)], 3: [(1, 1)]}
+        WE = "SSGGSSGG"
         for step in range(J + LA):
             if step < J:
                 stage1(step)
@@ -249,6 +257,11 @@ def tile_list_pigeon_bearing_support_kernel(
                         weave_w1(b + 1, a, half, WE[4 * b + 2 * a + half])
                         if half == 1:
                             quant_w1(b + 1, a, 1)
+            if step == J:
+                for h in range(2):
+                    yh.append(psum.tile([P, M], F32, name="yh_late", tag=f"z{h}", bufs=2))
+                for b, c, xc, xs in owed:
+                    second_pass(b, c, xc, xs, yh)
             if LG <= step < J + LG:
                 gathers(step - LG)
             if LA <= step:

@@ -19,11 +19,27 @@ ALU = mybir.AluOpType
 
 P = 128
 PACK = 4
-KP = P * PACK
-A = K // KP
-B = H // KP
-C = N // P
+SPAN = P * PACK
+K_PASSES = K // SPAN
+GROUPS = H // SPAN
+ROW_TILES = GROUPS * PACK
+OUT_TILES = N // P
 BANK = 512
+LAST = GROUPS - 1
+
+ANGLE_LAG = 3
+WINDOW_BUFS = 3
+PICKED_BUFS = ANGLE_LAG + 1
+
+W1_AFTER_GATHERS = {1: 1, 2: 4}
+X_AFTER_GATHERS = {0: 9, 1: ROW_TILES - 1}
+AFTER_GATHERS = set(W1_AFTER_GATHERS.values()) | set(X_AFTER_GATHERS.values())
+
+KIB = 1024
+WIDE_AT = [(2 + 6 * i) * KIB for i in range(3)]
+BEFORE, INSIDE = -2 * KIB, 2 * KIB
+SIN1_AT = WIDE_AT[2] + 8 * KIB
+LARGE_AT = [SIN1_AT + (8 + 8 * i) * KIB for i in range(4)]
 
 
 def tile_list_pigeon_bearing_support_kernel(
@@ -33,249 +49,327 @@ def tile_list_pigeon_bearing_support_kernel(
     with ExitStack() as ctx:
         held = ctx.enter_context(tc.tile_pool(name="held", bufs=1))
         ring = ctx.enter_context(tc.tile_pool(name="ring", bufs=2))
+        hand = ctx.enter_context(tc.tile_pool(name="hand", bufs=1))
         psum = ctx.enter_context(tc.psum_pool(name="psum", bufs=1))
 
         offs_t = held.tile([P, S // 16], U16, name="offs_t")
         pos1_t = held.tile([P, M // 16], U16, name="pos1_t")
         pos2_t = held.tile([P, M // 16], U16, name="pos2_t")
-        tabs = held.tile([P, T], U8, name="tabs", align_bytes=64)
-        vw = [held.tile([P, S], U32, name=f"vw{a}", align_bytes=64) for a in range(A)]
-        vs_raw = held.tile([P, S], U8, name="vs_raw", tag="vs_raw", align_bytes=64)
-        vs = held.tile([P, S], U8, name="vs", align_bytes=64)
-        w2s = held.tile([P, B, N], U8, name="w2s", align_bytes=64)
-        swing_t = held.tile([P, B, PACK], F32, name="swing_t")
-        ampo_t = held.tile([P, B, PACK], F32, name="ampo_t")
-        amph_t = held.tile([P, B, PACK], F32, name="amph_t")
-        seeds = [held.tile([P, 1], F32, name=f"seed{a}", tag=f"tabw{a}", align_bytes=64) for a in range(A)]
+        tab_s = held.tile([P, T], U8, name="tab_s", align_bytes=64)
+        v_codes = [held.tile([P, S], U32, name=f"v_codes{a}", align_bytes=64) for a in range(K_PASSES)]
+        v_picked_s = held.tile([P, S], U8, name="v_picked_s", align_bytes=64)
+        v_planes = held.tile([P, S], U8, name="v_planes", align_bytes=64)
+        w2_s = held.tile([P, GROUPS, N], U8, name="w2_s", align_bytes=64)
+        swing_t = held.tile([P, GROUPS, PACK], F32, name="swing_t")
+        amp_out_t = held.tile([P, GROUPS, PACK], F32, name="amp_out_t")
+        amp_home_t = held.tile([P, GROUPS, PACK], F32, name="amp_home_t")
         zero = held.tile([P, 1], F32, name="zero")
         half_pi = held.tile([P, 1], F32, name="half_pi")
 
-        nc.gpsimd.memset(seeds[1][:], 0.0)
-        nc.vector.memset(tabs[:].bitcast(I32), 0)
-        nc.vector.memset(seeds[0][:], 0.0)
-        nc.gpsimd.memset(w2s[:].rearrange("p b n -> p (b n)").bitcast(I32), 0)
-        nc.scalar.activation(out=zero[:], in_=seeds[1][:], func=ACT.Silu)
-        nc.vector.tensor_scalar(half_pi[:], seeds[0][:], math.pi / 2, None, ALU.add)
-        tabw = [held.tile([P, T], I32, name=f"tabw{a}", tag=f"tabw{a}", align_bytes=64) for a in range(A)]
+        seeds = [hand.tile([P, 16], F32, name=f"seed{i}", offset=LARGE_AT[2 * i + 1] - 32) for i in range(2)]
+        nc.gpsimd.memset(seeds[1][:, 0:1], 0.0)
+        nc.vector.memset(tab_s[:].bitcast(I32), 0)
+        nc.vector.memset(seeds[0][:, 0:1], 0.0)
+        nc.gpsimd.memset(w2_s[:].rearrange("p b n -> p (b n)").bitcast(I32), 0)
+        nc.scalar.activation(out=zero[:], in_=seeds[1][:, 0:1], func=ACT.Silu)
+        nc.vector.tensor_scalar(half_pi[:], seeds[0][:, 0:1], math.pi / 2, None, ALU.add)
 
-        w1raw = {}
+        tab_w = [
+            hand.tile([P, T], I32, name=f"tab_w{a}", align_bytes=64, offset=LARGE_AT[a]) for a in range(K_PASSES)
+        ]
+        w1_raw = {}
 
-        def load_w1(b, a):
-            rows = w1[a * KP : (a + 1) * KP, b * KP : (b + 1) * KP].rearrange("(p j) c -> p j c", j=PACK)
-            if b > 0 and a == 0:
-                raw = held.tile([P, PACK, KP], F32, name=f"w1late{b}", tag=f"tabw{b - 1}", align_bytes=64)
-                nc.sync.dma_start(raw[:], rows)
+        def load_w1(b):
+            for a in range(K_PASSES):
+                rows = w1[a * SPAN : (a + 1) * SPAN, b * SPAN : (b + 1) * SPAN].rearrange("(p i) c -> p i c", i=PACK)
+                place = LARGE_AT[2 * ((b + 1) % 2) + a]
+                shape = [P, 2, PACK, SPAN // 2] if b == 0 else [P, PACK, SPAN]
+                raw = hand.tile(shape, F32, name=f"w1_raw{b}{a}", align_bytes=64, offset=place)
                 for half in range(2):
-                    w1raw[b, a, half] = raw[:, :, half * 256 : half * 256 + 256]
-                return
-            for half in range(2):
-                raw = ring.tile([P, PACK, 256], F32, name="w1raw")
-                nc.sync.dma_start(raw[:], rows[:, :, half * 256 : half * 256 + 256])
-                w1raw[b, a, half] = raw[:]
+                    cols = slice(half * SPAN // 2, (half + 1) * SPAN // 2)
+                    if b == 0:
+                        w1_raw[b, a, half] = raw[:, half]
+                        nc.sync.dma_start(raw[:, half], rows[:, :, cols])
+                    else:
+                        w1_raw[b, a, half] = raw[:, :, cols]
+                if b > 0:
+                    nc.sync.dma_start(raw[:], rows)
 
         nc.sync.dma_start(offs_t[:], offs)
         nc.sync.dma_start(pos1_t[:], pos1)
         nc.sync.dma_start(pos2_t[:], pos2)
-        load_w1(0, 0)
-        for a in range(A):
-            for r in range(2):
-                nc.sync.dma_start(
-                    tabs[4 * a + r : P : 16, :].bitcast(I32), tab_scales[a, r:16:2, :].bitcast(I32)
-                )
-        for a in range(A):
-            nc.sync.dma_start(tabw[a][:], tab_words[a].rearrange("p t i -> p (t i)").bitcast(I32))
-        for vec, tile in ((swing, swing_t), (amp_out, ampo_t), (amp_home, amph_t)):
-            nc.gpsimd.dma_start(tile[:], vec.rearrange("(b p t) -> p b t", p=P, t=PACK))
-        for q in range(4):
+        for a in range(K_PASSES):
+            for u in range(2):
+                nc.sync.dma_start(tab_s[4 * a + u : P : 16, :].bitcast(I32), tab_scales[a, u:16:2, :].bitcast(I32))
+        for a in range(K_PASSES):
+            nc.sync.dma_start(tab_w[a][:], tab_words[a].rearrange("p t i -> p (t i)").bitcast(I32))
+        load_w1(0)
+        for vec, vec_t in ((swing, swing_t), (amp_out, amp_out_t), (amp_home, amp_home_t)):
+            nc.gpsimd.dma_start(vec_t[:], vec.rearrange("(b p t) -> p b t", p=P, t=PACK))
+        for d in range(4):
             nc.gpsimd.dma_start(
-                w2s[32 * q : 32 * q + 4].bitcast(I32),
-                w2_scales[:, 4 * q : 4 * q + 4, :].rearrange("b r n -> r b n").bitcast(I32),
+                w2_s[32 * d : 32 * d + 4].bitcast(I32),
+                w2_scales[:, 4 * d : 4 * d + 4, :].rearrange("b s n -> s b n").bitcast(I32),
             )
 
-        w1g, w1c, w1s = {}, {}, {}
-
-        def weave_w1(b, a, half, engine):
-            if half == 0:
-                w1g[b, a] = ring.tile([P, PACK * KP], BF16, name="w1g", align_bytes=64)
-            ms = slice(half * 64, half * 64 + 64)
-            src = w1raw[b, a, half].rearrange("p j (m t) -> p m j t", t=PACK)
-            dst = w1g[b, a][:].rearrange("p (t m j) -> p m j t", t=PACK, j=PACK)[:, ms]
-            if engine == "S":
-                nc.scalar.copy(dst, src)
-            elif engine == "V":
-                nc.vector.tensor_copy(dst, src)
-            else:
-                nc.gpsimd.tensor_scalar(
-                    dst.rearrange("p m j t -> p m t j"), src.rearrange("p m j t -> p m t j"), 1.0, 0.0, ALU.mult, ALU.add
-                )
-
-        def quant_w1(b, a, pieces):
-            w1c[b, a] = held.tile([P, KP], U32, name=f"w1c{b}{a}", align_bytes=64)
-            w1s[b, a] = held.tile([P, KP], U8, name=f"w1s{b}{a}", align_bytes=64)
-            width = KP // pieces
-            for i in range(pieces):
-                cols = slice(i * width, (i + 1) * width)
-                nc.vector.quantize_mx(
-                    out=w1c[b, a][:, cols].bitcast(FP8X4),
-                    scales=w1s[b, a][:, cols],
-                    in_=w1g[b, a][:, PACK * i * width : PACK * (i + 1) * width],
-                )
-
-        weave_w1(0, 0, 0, "S")
-        weave_w1(0, 0, 1, "S")
-        load_w1(0, 1)
-
-        nc.vector.tensor_copy(vs_raw[:], tabs[:].indirect(offs_t[:]))
-        nc.vector.tensor_copy(vs[:].bitcast(I32), vs_raw[:].bitcast(I32))
-        for a in range(A):
-            for r in range(2):
+        nc.vector.tensor_copy(v_picked_s[:], tab_s[:].indirect(offs_t[:]))
+        nc.vector.tensor_copy(v_planes[:].bitcast(I32), v_picked_s[:].bitcast(I32))
+        for a in range(K_PASSES):
+            for u in range(2):
                 nc.scalar.dma_start(
-                    vs[4 * a + 2 + r : P : 32, :].bitcast(I32), vs_raw[16 + 4 * a + r : P : 32, :].bitcast(I32)
+                    v_planes[4 * a + 2 + u : P : 32, :].bitcast(I32),
+                    v_picked_s[16 + 4 * a + u : P : 32, :].bitcast(I32),
                 )
-        nc.vector.tensor_copy(vw[0][:], tabw[0][:].bitcast(U32).indirect(offs_t[:]))
-        quant_w1(0, 0, 1)
-        nc.vector.tensor_copy(vw[1][:], tabw[1][:].bitcast(U32).indirect(offs_t[:]))
-        weave_w1(0, 1, 0, "S")
-        weave_w1(0, 1, 1, "V")
-        quant_w1(0, 1, PACK)
-        w2w = held.tile([P, B, 2 * N], U8, name="w2w", tag="vs_raw", align_bytes=64)
-        nc.sync.dma_start(w2w[:].bitcast(I32), w2_words.rearrange("b p c -> p b c").bitcast(I32))
+        for a in range(K_PASSES):
+            nc.vector.tensor_copy(v_codes[a][:], tab_w[a][:].bitcast(U32).indirect(offs_t[:]))
 
-        windows = {}
+        w1_codes, w1_planes, w1_wide = {}, {}, {}
 
-        def stage1(j):
+        def gpsimd_move(dst, src):
+            nc.gpsimd.tensor_scalar(dst, src, 1.0, 0.0, ALU.mult, ALU.add)
+
+        def weave_w1(b, a, half, woven, move):
+            words = slice(half * P // 2, (half + 1) * P // 2)
+            if move is gpsimd_move:
+                dst = woven.rearrange("p (t q i) -> p q t i", t=PACK, i=PACK)
+                src = w1_raw[b, a, half].rearrange("p i (q t) -> p q t i", t=PACK)
+            else:
+                dst = woven.rearrange("p (u e q i) -> p q u i e", u=2, e=2, i=PACK)
+                src = w1_raw[b, a, half].rearrange("p i (q u e) -> p q u i e", u=2, e=2)
+            move(dst[:, words], src)
+
+        for a in range(K_PASSES):
+            woven = held.tile([P, PACK * SPAN], BF16, name="w1_woven", tag=f"w1_woven{a}", align_bytes=64)
+            weave_w1(0, a, 0, woven[:], nc.scalar.copy)
+            weave_w1(0, a, 1, woven[:], nc.vector.tensor_copy)
+            w1_codes[0, a] = held.tile([P, SPAN], U32, name=f"w1_codes0{a}", align_bytes=64)
+            w1_planes[0, a] = held.tile([P, SPAN], U8, name=f"w1_planes0{a}", align_bytes=64)
+            width = P if a == K_PASSES - 1 else SPAN
+            for first in range(0, SPAN, width):
+                nc.vector.quantize_mx(
+                    out=w1_codes[0, a][:, first : first + width].bitcast(FP8X4),
+                    scales=w1_planes[0, a][:, first : first + width],
+                    in_=woven[:, PACK * first : PACK * (first + width)],
+                )
+
+        w2_w = held.tile([P, GROUPS, 2 * N], U8, name="w2_w", tag=f"w1_woven{K_PASSES - 1}", align_bytes=64)
+        nc.sync.dma_start(w2_w[:].bitcast(I32), w2_words.rearrange("b p c -> p b c").bitcast(I32))
+
+        def weave_w1_group(b):
+            w1_wide[b] = hand.tile(
+                [P, K_PASSES * PACK * SPAN], BF16, name=f"w1_wide{b}", align_bytes=64, offset=WIDE_AT[b - 1]
+            )
+            for a in range(K_PASSES):
+                for half in range(2):
+                    move = nc.scalar.copy if (b, a, half) == (1, 0, 0) else gpsimd_move
+                    weave_w1(b, a, half, w1_wide[b][:, a * PACK * SPAN : (a + 1) * PACK * SPAN], move)
+
+        def quantise_w1_group(b):
+            codes = held.tile(
+                [P, K_PASSES * SPAN], U32, name=f"w1_codes{b}", tag=f"after{W1_AFTER_GATHERS[b]}", align_bytes=64
+            )
+            planes = held.tile([P, K_PASSES * SPAN], U8, name=f"w1_planes{b}", align_bytes=64)
+            nc.vector.quantize_mx(out=codes[:].bitcast(FP8X4), scales=planes[:], in_=w1_wide[b][:])
+            for a in range(K_PASSES):
+                w1_codes[b, a] = codes[:, a * SPAN : (a + 1) * SPAN]
+                w1_planes[b, a] = planes[:, a * SPAN : (a + 1) * SPAN]
+
+        windows, picked, sines, abs_h, out_rows = {}, {}, {}, {}, {}
+
+        def first_product(j):
             b, t = divmod(j, PACK)
-            win = ring.tile([P, S], F32, name="win", bufs=4)
-            cols = slice(t * P, (t + 1) * P)
-            for h in range(S // BANK):
-                z = psum.tile([P, BANK], F32, name="z", tag=f"z{h}", bufs=2)
-                hs = slice(h * BANK, (h + 1) * BANK)
-                for a in range(A):
+            if j in AFTER_GATHERS:
+                windows[j] = held.tile([P, S], F32, name="window", tag=f"after{j}", align_bytes=64)
+            else:
+                windows[j] = ring.tile([P, S], F32, name="window", bufs=WINDOW_BUFS)
+            rows = slice(t * P, (t + 1) * P)
+            for half in range(S // BANK):
+                z = psum.tile([P, BANK], F32, name="z", tag=f"z{half}", bufs=2)
+                cols = slice(half * BANK, (half + 1) * BANK)
+                for a in range(K_PASSES):
                     nc.tensor.matmul_mx(
                         out=z[:],
-                        lhsT=w1c[b, a][:, cols].bitcast(FP8X4),
-                        lhsT_scale=w1s[b, a][:, cols],
-                        rhs=vw[a][:, hs].bitcast(FP8X4),
-                        rhs_scale=vs[4 * a : P, hs],
+                        lhsT=w1_codes[b, a][:, rows].bitcast(FP8X4),
+                        lhsT_scale=w1_planes[b, a][:, rows],
+                        rhs=v_codes[a][:, cols].bitcast(FP8X4),
+                        rhs_scale=v_planes[4 * a : P, cols],
                         start=(a == 0),
-                        stop=(a == A - 1),
+                        stop=(a == K_PASSES - 1),
                     )
-                nc.scalar.activation(out=win[:, hs], in_=z[:], func=ACT.Tanh, bias=zero[:])
-            windows[j] = win
+                nc.scalar.activation(out=windows[j][:, cols], in_=z[:], func=ACT.Tanh, bias=zero[:])
 
-        gh, go, so, ah = {}, {}, {}, {}
+        picked_at = {
+            W1_AFTER_GATHERS[1] + 1: WIDE_AT[0] + BEFORE,
+            W1_AFTER_GATHERS[2] + 1: WIDE_AT[1] + BEFORE,
+            X_AFTER_GATHERS[0] + 1: SIN1_AT,
+        }
 
         def gathers(j):
-            b, t = divmod(j, PACK)
-            if t == 0:
-                gh[b] = ring.tile([P, PACK, M], F32, name="gh")
-                go[b] = ring.tile([P, PACK, M], F32, name="go")
-            nc.vector.tensor_copy(go[b][:, t, :], windows[j][:].indirect(pos1_t[:]))
-            nc.vector.tensor_copy(gh[b][:, t, :], windows[j][:].indirect(pos2_t[:]))
+            if j in picked_at:
+                picked[j] = hand.tile([P, 2, M], F32, name=f"picked{j}", align_bytes=64, offset=picked_at[j])
+            else:
+                picked[j] = ring.tile([P, 2, M], F32, name="picked", bufs=PICKED_BUFS)
+            nc.vector.tensor_copy(picked[j][:, 0, :], windows[j][:].indirect(pos1_t[:]))
+            nc.vector.tensor_copy(picked[j][:, 1, :], windows[j][:].indirect(pos2_t[:]))
 
         def angles(j):
             b, t = divmod(j, PACK)
             if t == 0:
-                ah[b] = ring.tile([P, PACK, M], F32, name="ah")
-                so[b] = ring.tile([P, PACK, M], F32, name="so")
-            sw = swing_t[:, b, t : t + 1]
-            nc.scalar.activation(out=so[b][:, t, :], in_=go[b][:, t, :], func=ACT.Sin, scale=sw, bias=zero[:])
-            nc.scalar.activation(out=ah[b][:, t, :], in_=gh[b][:, t, :], func=ACT.Abs, scale=sw, bias=zero[:])
+                abs_h[b] = ring.tile([P, PACK, M], F32, name="abs_h")
+                if b == 1:
+                    sines[b] = hand.tile([P, PACK, M], F32, name="sines1", align_bytes=64, offset=SIN1_AT)
+                else:
+                    sines[b] = ring.tile([P, PACK, M], F32, name="sines", bufs=1)
+                if b == LAST:
+                    out_rows[b] = ring.tile([P, PACK, M], BF16, name="out_rows", bufs=1)
+            gain = swing_t[:, b, t : t + 1]
+            nc.scalar.activation(out=sines[b][:, t, :], in_=picked[j][:, 0, :], func=ACT.Sin, scale=gain, bias=zero[:])
+            if b == LAST:
+                nc.scalar.activation(
+                    out=out_rows[b][:, t, :], in_=sines[b][:, t, :], func=ACT.Copy, scale=amp_out_t[:, b, t : t + 1]
+                )
+            nc.scalar.activation(out=abs_h[b][:, t, :], in_=picked[j][:, 1, :], func=ACT.Abs, scale=gain, bias=zero[:])
 
-        yo = [psum.tile([P, M], F32, name=f"yo{c}") for c in range(C)]
-        yh = [psum.tile([P, M], F32, name="yh0")]
+        y_out = [psum.tile([P, M], F32, name=f"y_out{c}") for c in range(OUT_TILES)]
+        y_home = [psum.tile([P, M], F32, name="y_home0")]
         owed = []
 
-        def second_pass(b, c, xc, xs, y):
+        def second_pass(b, c, y, codes, planes, stop):
             nc.tensor.matmul_mx(
-                out=y[c][:],
-                lhsT=w2w[:, b, 2 * P * c : 2 * P * (c + 1)].bitcast(FP4X4),
-                lhsT_scale=w2s[:, b, P * c : P * (c + 1)],
-                rhs=xc[:].bitcast(FP8X4),
-                rhs_scale=xs[:],
+                out=y,
+                lhsT=w2_w[:, b, 2 * P * c : 2 * P * (c + 1)].bitcast(FP4X4),
+                lhsT_scale=w2_s[:, b, P * c : P * (c + 1)],
+                rhs=codes.bitcast(FP8X4),
+                rhs_scale=planes,
                 start=(b == 0),
-                stop=(b == B - 1),
+                stop=stop,
             )
 
-        def stage2(b, x, y):
-            leg = "o" if y is yo else "h"
-            xc = ring.tile([P, M], U32, name="xc", tag=f"xc{leg}", align_bytes=64, bufs=B)
-            xs = ring.tile([P, M], U8, name="xs", tag=f"xs{leg}", align_bytes=64, bufs=B)
-            nc.vector.quantize_mx(out=xc[:].bitcast(FP8X4), scales=xs[:], in_=x[:])
-            for c in range(C):
-                if c < len(y):
-                    second_pass(b, c, xc, xs, y)
+        def second_passes(b, ys, codes, planes):
+            for c in range(OUT_TILES):
+                if c < len(ys):
+                    second_pass(b, c, ys[c][:], codes, planes, b == LAST)
                 else:
-                    owed.append((b, c, xc, xs))
+                    owed.append((b, c, codes, planes))
 
-        def finish_home(b):
-            ch = ring.tile([P, M, PACK], F32, name="ch", bufs=1)
+        def home_leg(b, xh, engine):
+            cosines = ring.tile([P, M, PACK], F32, name="cosines")
             for half in range(2):
-                ms = slice(half * 256, half * 256 + 256)
+                pairs = slice(half * M // 4, (half + 1) * M // 4)
                 nc.scalar.activation(
-                    out=ch[:, ms, :],
-                    in_=ah[b][:].rearrange("p t m -> p m t")[:, ms, :],
+                    out=cosines[:].rearrange("p (c i) t -> p c t i", i=2)[:, pairs],
+                    in_=abs_h[b][:].rearrange("p t (c i) -> p c t i", i=2)[:, pairs],
                     func=ACT.Sin,
                     scale=-1.0,
                     bias=half_pi[:],
                 )
-            xh = ring.tile([P, M * PACK], BF16, name="xh", align_bytes=64)
-            xv = xh[:].rearrange("p (m t) -> p m t", t=PACK)
-            if b in (0, 1):
-                for half in range(2):
-                    ms = slice(half * 256, half * 256 + 256)
-                    nc.gpsimd.tensor_tensor(
-                        xv[:, ms, :], ch[:, ms, :], amph_t[:, b, :].unsqueeze(1).to_broadcast([P, 256, PACK]), ALU.mult
-                    )
-            else:
-                nc.vector.tensor_tensor(xv, ch[:], amph_t[:, b, :].unsqueeze(1).to_broadcast([P, M, PACK]), ALU.mult)
-            return xh
+            for half in range(2):
+                cols = slice(half * M // 2, (half + 1) * M // 2)
+                engine.tensor_tensor(
+                    xh.rearrange("p (m t) -> p m t", t=PACK)[:, cols, :],
+                    cosines[:, cols, :],
+                    amp_home_t[:, b, :].unsqueeze(1).to_broadcast([P, M // 2, PACK]),
+                    ALU.mult,
+                )
 
-        def finish_out(b):
-            xo = ring.tile([P, M * PACK], BF16, name="xo", align_bytes=64)
+        x_tiles = {}
+
+        def legs_of_group_0():
+            x = hand.tile([P, 2 * PACK * M], BF16, name="x_wide", align_bytes=64, offset=WIDE_AT[2])
+            out_rows[0] = hand.tile([P, PACK, M], BF16, name="out_rows0", align_bytes=64, offset=WIDE_AT[1] + INSIDE)
+            for t in range(PACK):
+                nc.gpsimd.tensor_scalar(
+                    out_rows[0][:, t, :], sines[0][:, t, :], amp_out_t[:, 0, t : t + 1], 0.0, ALU.mult, ALU.add
+                )
+            for half in range(2):
+                cols = slice(half * M // 2, (half + 1) * M // 2)
+                gpsimd_move(
+                    x[:, : PACK * M].rearrange("p (m t) -> p m t", t=PACK)[:, cols],
+                    out_rows[0][:].rearrange("p t m -> p m t")[:, cols],
+                )
+            home_leg(0, x[:, PACK * M :], nc.gpsimd)
+            x_tiles[0] = [x[:]]
+
+        def legs_of_group_1():
+            xo = hand.tile([P, PACK * M], BF16, name="xo1", align_bytes=64, offset=WIDE_AT[2] + INSIDE)
+            xh = hand.tile([P, PACK * M], BF16, name="xh1", align_bytes=64, offset=SIN1_AT + 4 * KIB)
             nc.vector.tensor_tensor(
                 xo[:].rearrange("p (c i t) -> p c t i", i=4, t=PACK),
-                so[b][:].rearrange("p t (c i) -> p c t i", i=4),
-                ampo_t[:, b, :].unsqueeze(1).unsqueeze(3).to_broadcast([P, M // 4, PACK, 4]),
+                sines[1][:].rearrange("p t (c i) -> p c t i", i=4),
+                amp_out_t[:, 1, :].unsqueeze(1).unsqueeze(3).to_broadcast([P, M // 4, PACK, 4]),
                 ALU.mult,
             )
-            return xo
+            home_leg(1, xh[:], nc.gpsimd)
+            x_tiles[1] = [xo[:], xh[:]]
 
-        J = B * PACK
-        LG, LA = 1, 3
-        WP = {0: [(0, 0)], 1: [(0, 1)], 2: [(1, 0)], 3: [(1, 1)]}
-        WE = "SSGGSSGG"
-        for step in range(J + LA):
-            if step < J:
-                stage1(step)
+        def quantise_legs(b):
+            codes = held.tile([P, 2 * M], U32, name="x_codes", tag=f"after{X_AFTER_GATHERS[b]}", align_bytes=64)
+            planes = ring.tile([P, 2 * M], U8, name="x_planes", align_bytes=64)
+            width = 2 * M // len(x_tiles[b])
+            for i, x in enumerate(x_tiles[b]):
+                cols = slice(i * width, (i + 1) * width)
+                nc.vector.quantize_mx(out=codes[:, cols].bitcast(FP8X4), scales=planes[:, cols], in_=x)
+            second_passes(b, y_out, codes[:, :M], planes[:, :M])
+            second_passes(b, y_home, codes[:, M:], planes[:, M:])
+
+        def legs_of_last_group():
+            xo = ring.tile([P, PACK * M], BF16, name="xo", tag="x_last", align_bytes=64)
+            nc.vector.tensor_copy(
+                xo[:].rearrange("p (c i t) -> p c t i", i=4, t=PACK),
+                out_rows[LAST][:].rearrange("p t (c i) -> p c t i", i=4),
+            )
+            codes = ring.tile([P, M], U32, name="xo_codes", tag="last_codes", align_bytes=64)
+            planes = ring.tile([P, M], U8, name="xo_planes", tag="last_planes", align_bytes=64)
+            nc.vector.quantize_mx(out=codes[:].bitcast(FP8X4), scales=planes[:], in_=xo[:])
+            second_passes(LAST, y_out, codes[:], planes[:])
+
+            xh = ring.tile([P, PACK * M], BF16, name="xh", tag="x_last", align_bytes=64)
+            home_leg(LAST, xh[:], nc.vector)
+            codes = ring.tile([P, M], U32, name="xh_codes", tag="last_codes", align_bytes=64)
+            planes = ring.tile([P, M], U8, name="xh_planes", tag="last_planes", align_bytes=64)
+            for first in range(0, M, M // 2):
+                cols = slice(first, first + M // 2)
+                nc.vector.quantize_mx(
+                    out=codes[:, cols].bitcast(FP8X4),
+                    scales=planes[:, cols],
+                    in_=xh[:, PACK * first : PACK * (first + M // 2)],
+                )
+                for c in range(OUT_TILES):
+                    for m0 in range(first, first + M // 2, P):
+                        part = slice(m0, m0 + P)
+                        second_pass(LAST, c, y_home[c][:, part], codes[:, part], planes[:, part], m0 + P == M)
+
+        legs = [legs_of_group_0, legs_of_group_1, legs_of_last_group]
+
+        for step in range(ROW_TILES + ANGLE_LAG):
+            if step < ROW_TILES:
+                first_product(step)
                 b, t = divmod(step, PACK)
-                if b + 1 < B:
-                    if t == 0:
-                        load_w1(b + 1, 0)
-                        load_w1(b + 1, 1)
-                    for a, half in WP.get(t, []):
-                        weave_w1(b + 1, a, half, WE[4 * b + 2 * a + half])
-                        if half == 1:
-                            quant_w1(b + 1, a, 1)
-            if step == J:
-                for h in range(2):
-                    yh.append(psum.tile([P, M], F32, name="yh_late", tag=f"z{h}", bufs=2))
-                for b, c, xc, xs in owed:
-                    second_pass(b, c, xc, xs, yh)
-            if LG <= step < J + LG:
-                gathers(step - LG)
-            if LA <= step:
-                angles(step - LA)
-                b, t = divmod(step - LA, PACK)
+                if t == 0 and b < LAST:
+                    load_w1(b + 1)
+                    weave_w1_group(b + 1)
+            if step == ROW_TILES:
+                for half in range(2):
+                    y_home.append(psum.tile([P, M], F32, name="y_home", tag=f"z{half}", bufs=2))
+                for b, c, codes, planes in owed:
+                    second_pass(b, c, y_home[c][:], codes, planes, False)
+            if 1 <= step <= ROW_TILES:
+                gathers(step - 1)
+                for b, j in W1_AFTER_GATHERS.items():
+                    if j == step - 1:
+                        quantise_w1_group(b)
+                for b, j in X_AFTER_GATHERS.items():
+                    if j == step - 1:
+                        quantise_legs(b)
+            if step >= ANGLE_LAG:
+                angles(step - ANGLE_LAG)
+                b, t = divmod(step - ANGLE_LAG, PACK)
                 if t == PACK - 1:
-                    xo = finish_out(b)
-                    xh = finish_home(b)
-                    stage2(b, xo, yo)
-                    stage2(b, xh, yh)
+                    legs[b]()
 
-        for c in range(C):
-            yo_sb = ring.tile([P, M], F32, name="yo_sb", bufs=3)
-            nc.scalar.copy(yo_sb[:], yo[c][:])
-            res = ring.tile([P, M], F32, name="res", bufs=3)
-            nc.vector.tensor_tensor(res[:], yh[c][:], yo_sb[:], ALU.max)
-            nc.sync.dma_start(out[c * P : (c + 1) * P, :], res[:])
+        for c in range(OUT_TILES):
+            y_out_sb = ring.tile([P, M], F32, name="y_out_sb", bufs=OUT_TILES)
+            nc.scalar.copy(y_out_sb[:], y_out[c][:])
+            result = ring.tile([P, M], F32, name="result", bufs=OUT_TILES)
+            nc.vector.tensor_tensor(result[:], y_home[c][:], y_out_sb[:], ALU.max)
+            nc.sync.dma_start(out[c * P : (c + 1) * P, :], result[:])

import math
from contextlib import ExitStack

import concourse.mybir as mybir

K, T, S, M, H, N = 1024, 2048, 1024, 512, 1536, 384
FLOPS = 2 * K * H * S + 2 * 2 * H * N * M

F32 = mybir.dt.float32
BF16 = mybir.dt.bfloat16
I32 = mybir.dt.int32
U32 = mybir.dt.uint32
U16 = mybir.dt.uint16
U8 = mybir.dt.uint8
FP8X4 = mybir.dt.float8_e4m3fn_x4
FP4X4 = mybir.dt.float4_e2m1fn_x4
ACT = mybir.ActivationFunctionType
ALU = mybir.AluOpType

P = 128
PACK = 4
SPAN = P * PACK
K_PASSES = K // SPAN
GROUPS = H // SPAN
ROW_TILES = GROUPS * PACK
OUT_TILES = N // P
BANK = 512
LAST = GROUPS - 1

ANGLE_LAG = 3
WINDOW_BUFS = 3
PICKED_BUFS = ANGLE_LAG + 1

W1_AFTER_GATHERS = {1: 1, 2: 4}
X_AFTER_GATHERS = {0: 9, 1: ROW_TILES - 1}
AFTER_GATHERS = set(W1_AFTER_GATHERS.values()) | set(X_AFTER_GATHERS.values())

KIB = 1024
WIDE_AT = [(2 + 6 * i) * KIB for i in range(3)]
BEFORE, INSIDE = -2 * KIB, 2 * KIB
SIN1_AT = WIDE_AT[2] + 8 * KIB
LARGE_AT = [SIN1_AT + (8 + 8 * i) * KIB for i in range(4)]


def tile_list_pigeon_bearing_support_kernel(
    tc, tab_words, tab_scales, offs, pos1, pos2, w1, swing, amp_out, amp_home, w2_words, w2_scales, out
):
    nc = tc.nc
    with ExitStack() as ctx:
        held = ctx.enter_context(tc.tile_pool(name="held", bufs=1))
        ring = ctx.enter_context(tc.tile_pool(name="ring", bufs=2))
        hand = ctx.enter_context(tc.tile_pool(name="hand", bufs=1))
        psum = ctx.enter_context(tc.psum_pool(name="psum", bufs=1))

        offs_t = held.tile([P, S // 16], U16, name="offs_t")
        pos1_t = held.tile([P, M // 16], U16, name="pos1_t")
        pos2_t = held.tile([P, M // 16], U16, name="pos2_t")
        tab_s = held.tile([P, T], U8, name="tab_s", align_bytes=64)
        v_codes = [held.tile([P, S], U32, name=f"v_codes{a}", align_bytes=64) for a in range(K_PASSES)]
        v_picked_s = held.tile([P, S], U8, name="v_picked_s", align_bytes=64)
        v_planes = held.tile([P, S], U8, name="v_planes", align_bytes=64)
        w2_s = held.tile([P, GROUPS, N], U8, name="w2_s", align_bytes=64)
        swing_t = held.tile([P, GROUPS, PACK], F32, name="swing_t")
        amp_out_t = held.tile([P, GROUPS, PACK], F32, name="amp_out_t")
        amp_home_t = held.tile([P, GROUPS, PACK], F32, name="amp_home_t")
        zero = held.tile([P, 1], F32, name="zero")
        half_pi = held.tile([P, 1], F32, name="half_pi")

        seeds = [hand.tile([P, 16], F32, name=f"seed{i}", offset=LARGE_AT[2 * i + 1] - 32) for i in range(2)]
        nc.gpsimd.memset(seeds[1][:, 0:1], 0.0)
        nc.vector.memset(tab_s[:].bitcast(I32), 0)
        nc.vector.memset(seeds[0][:, 0:1], 0.0)
        nc.gpsimd.memset(w2_s[:].rearrange("p b n -> p (b n)").bitcast(I32), 0)
        nc.scalar.activation(out=zero[:], in_=seeds[1][:, 0:1], func=ACT.Silu)
        nc.vector.tensor_scalar(half_pi[:], seeds[0][:, 0:1], math.pi / 2, None, ALU.add)

        tab_w = [
            hand.tile([P, T], I32, name=f"tab_w{a}", align_bytes=64, offset=LARGE_AT[a]) for a in range(K_PASSES)
        ]
        w1_raw = {}

        def load_w1(b):
            for a in range(K_PASSES):
                rows = w1[a * SPAN : (a + 1) * SPAN, b * SPAN : (b + 1) * SPAN].rearrange("(p i) c -> p i c", i=PACK)
                place = LARGE_AT[2 * ((b + 1) % 2) + a]
                shape = [P, 2, PACK, SPAN // 2] if b == 0 else [P, PACK, SPAN]
                raw = hand.tile(shape, F32, name=f"w1_raw{b}{a}", align_bytes=64, offset=place)
                for half in range(2):
                    cols = slice(half * SPAN // 2, (half + 1) * SPAN // 2)
                    if b == 0:
                        w1_raw[b, a, half] = raw[:, half]
                        nc.sync.dma_start(raw[:, half], rows[:, :, cols])
                    else:
                        w1_raw[b, a, half] = raw[:, :, cols]
                if b > 0:
                    nc.sync.dma_start(raw[:], rows)

        nc.sync.dma_start(offs_t[:], offs)
        nc.sync.dma_start(pos1_t[:], pos1)
        nc.sync.dma_start(pos2_t[:], pos2)
        for a in range(K_PASSES):
            for u in range(2):
                nc.sync.dma_start(tab_s[4 * a + u : P : 16, :].bitcast(I32), tab_scales[a, u:16:2, :].bitcast(I32))
        for a in range(K_PASSES):
            nc.sync.dma_start(tab_w[a][:], tab_words[a].rearrange("p t i -> p (t i)").bitcast(I32))
        load_w1(0)
        for vec, vec_t in ((swing, swing_t), (amp_out, amp_out_t), (amp_home, amp_home_t)):
            nc.gpsimd.dma_start(vec_t[:], vec.rearrange("(b p t) -> p b t", p=P, t=PACK))
        for d in range(4):
            nc.gpsimd.dma_start(
                w2_s[32 * d : 32 * d + 4].bitcast(I32),
                w2_scales[:, 4 * d : 4 * d + 4, :].rearrange("b s n -> s b n").bitcast(I32),
            )

        nc.vector.tensor_copy(v_picked_s[:], tab_s[:].indirect(offs_t[:]))
        nc.vector.tensor_copy(v_planes[:].bitcast(I32), v_picked_s[:].bitcast(I32))
        for a in range(K_PASSES):
            for u in range(2):
                nc.scalar.dma_start(
                    v_planes[4 * a + 2 + u : P : 32, :].bitcast(I32),
                    v_picked_s[16 + 4 * a + u : P : 32, :].bitcast(I32),
                )
        for a in range(K_PASSES):
            nc.vector.tensor_copy(v_codes[a][:], tab_w[a][:].bitcast(U32).indirect(offs_t[:]))

        w1_codes, w1_planes, w1_wide = {}, {}, {}

        def gpsimd_move(dst, src):
            nc.gpsimd.tensor_scalar(dst, src, 1.0, 0.0, ALU.mult, ALU.add)

        def weave_w1(b, a, half, woven, move):
            words = slice(half * P // 2, (half + 1) * P // 2)
            if move is gpsimd_move:
                dst = woven.rearrange("p (t q i) -> p q t i", t=PACK, i=PACK)
                src = w1_raw[b, a, half].rearrange("p i (q t) -> p q t i", t=PACK)
            else:
                dst = woven.rearrange("p (u e q i) -> p q u i e", u=2, e=2, i=PACK)
                src = w1_raw[b, a, half].rearrange("p i (q u e) -> p q u i e", u=2, e=2)
            move(dst[:, words], src)

        for a in range(K_PASSES):
            woven = held.tile([P, PACK * SPAN], BF16, name="w1_woven", tag=f"w1_woven{a}", align_bytes=64)
            weave_w1(0, a, 0, woven[:], nc.scalar.copy)
            weave_w1(0, a, 1, woven[:], nc.vector.tensor_copy)
            w1_codes[0, a] = held.tile([P, SPAN], U32, name=f"w1_codes0{a}", align_bytes=64)
            w1_planes[0, a] = held.tile([P, SPAN], U8, name=f"w1_planes0{a}", align_bytes=64)
            width = P if a == K_PASSES - 1 else SPAN
            for first in range(0, SPAN, width):
                nc.vector.quantize_mx(
                    out=w1_codes[0, a][:, first : first + width].bitcast(FP8X4),
                    scales=w1_planes[0, a][:, first : first + width],
                    in_=woven[:, PACK * first : PACK * (first + width)],
                )

        w2_w = held.tile([P, GROUPS, 2 * N], U8, name="w2_w", tag=f"w1_woven{K_PASSES - 1}", align_bytes=64)
        nc.sync.dma_start(w2_w[:].bitcast(I32), w2_words.rearrange("b p c -> p b c").bitcast(I32))

        def weave_w1_group(b):
            w1_wide[b] = hand.tile(
                [P, K_PASSES * PACK * SPAN], BF16, name=f"w1_wide{b}", align_bytes=64, offset=WIDE_AT[b - 1]
            )
            for a in range(K_PASSES):
                for half in range(2):
                    move = nc.scalar.copy if (b, a, half) == (1, 0, 0) else gpsimd_move
                    weave_w1(b, a, half, w1_wide[b][:, a * PACK * SPAN : (a + 1) * PACK * SPAN], move)

        def quantise_w1_group(b):
            codes = held.tile(
                [P, K_PASSES * SPAN], U32, name=f"w1_codes{b}", tag=f"after{W1_AFTER_GATHERS[b]}", align_bytes=64
            )
            planes = held.tile([P, K_PASSES * SPAN], U8, name=f"w1_planes{b}", align_bytes=64)
            nc.vector.quantize_mx(out=codes[:].bitcast(FP8X4), scales=planes[:], in_=w1_wide[b][:])
            for a in range(K_PASSES):
                w1_codes[b, a] = codes[:, a * SPAN : (a + 1) * SPAN]
                w1_planes[b, a] = planes[:, a * SPAN : (a + 1) * SPAN]

        windows, picked, sines, abs_h, out_rows = {}, {}, {}, {}, {}

        def first_product(j):
            b, t = divmod(j, PACK)
            if j in AFTER_GATHERS:
                windows[j] = held.tile([P, S], F32, name="window", tag=f"after{j}", align_bytes=64)
            else:
                windows[j] = ring.tile([P, S], F32, name="window", bufs=WINDOW_BUFS)
            rows = slice(t * P, (t + 1) * P)
            for half in range(S // BANK):
                z = psum.tile([P, BANK], F32, name="z", tag=f"z{half}", bufs=2)
                cols = slice(half * BANK, (half + 1) * BANK)
                for a in range(K_PASSES):
                    nc.tensor.matmul_mx(
                        out=z[:],
                        lhsT=w1_codes[b, a][:, rows].bitcast(FP8X4),
                        lhsT_scale=w1_planes[b, a][:, rows],
                        rhs=v_codes[a][:, cols].bitcast(FP8X4),
                        rhs_scale=v_planes[4 * a : P, cols],
                        start=(a == 0),
                        stop=(a == K_PASSES - 1),
                    )
                nc.scalar.activation(out=windows[j][:, cols], in_=z[:], func=ACT.Tanh, bias=zero[:])

        picked_at = {
            W1_AFTER_GATHERS[1] + 1: WIDE_AT[0] + BEFORE,
            W1_AFTER_GATHERS[2] + 1: WIDE_AT[1] + BEFORE,
            X_AFTER_GATHERS[0] + 1: SIN1_AT,
        }

        def gathers(j):
            if j in picked_at:
                picked[j] = hand.tile([P, 2, M], F32, name=f"picked{j}", align_bytes=64, offset=picked_at[j])
            else:
                picked[j] = ring.tile([P, 2, M], F32, name="picked", bufs=PICKED_BUFS)
            nc.vector.tensor_copy(picked[j][:, 0, :], windows[j][:].indirect(pos1_t[:]))
            nc.vector.tensor_copy(picked[j][:, 1, :], windows[j][:].indirect(pos2_t[:]))

        def angles(j):
            b, t = divmod(j, PACK)
            if t == 0:
                abs_h[b] = ring.tile([P, PACK, M], F32, name="abs_h")
                if b == 1:
                    sines[b] = hand.tile([P, PACK, M], F32, name="sines1", align_bytes=64, offset=SIN1_AT)
                else:
                    sines[b] = ring.tile([P, PACK, M], F32, name="sines", bufs=1)
                if b == LAST:
                    out_rows[b] = ring.tile([P, PACK, M], BF16, name="out_rows", bufs=1)
            gain = swing_t[:, b, t : t + 1]
            nc.scalar.activation(out=sines[b][:, t, :], in_=picked[j][:, 0, :], func=ACT.Sin, scale=gain, bias=zero[:])
            if b == LAST:
                nc.scalar.activation(
                    out=out_rows[b][:, t, :], in_=sines[b][:, t, :], func=ACT.Copy, scale=amp_out_t[:, b, t : t + 1]
                )
            nc.scalar.activation(out=abs_h[b][:, t, :], in_=picked[j][:, 1, :], func=ACT.Abs, scale=gain, bias=zero[:])

        y_out = [psum.tile([P, M], F32, name=f"y_out{c}") for c in range(OUT_TILES)]
        y_home = [psum.tile([P, M], F32, name="y_home0")]
        owed = []

        def second_pass(b, c, y, codes, planes, stop):
            nc.tensor.matmul_mx(
                out=y,
                lhsT=w2_w[:, b, 2 * P * c : 2 * P * (c + 1)].bitcast(FP4X4),
                lhsT_scale=w2_s[:, b, P * c : P * (c + 1)],
                rhs=codes.bitcast(FP8X4),
                rhs_scale=planes,
                start=(b == 0),
                stop=stop,
            )

        def second_passes(b, ys, codes, planes):
            for c in range(OUT_TILES):
                if c < len(ys):
                    second_pass(b, c, ys[c][:], codes, planes, b == LAST)
                else:
                    owed.append((b, c, codes, planes))

        def home_leg(b, xh, engine):
            cosines = ring.tile([P, M, PACK], F32, name="cosines")
            for half in range(2):
                pairs = slice(half * M // 4, (half + 1) * M // 4)
                nc.scalar.activation(
                    out=cosines[:].rearrange("p (c i) t -> p c t i", i=2)[:, pairs],
                    in_=abs_h[b][:].rearrange("p t (c i) -> p c t i", i=2)[:, pairs],
                    func=ACT.Sin,
                    scale=-1.0,
                    bias=half_pi[:],
                )
            for half in range(2):
                cols = slice(half * M // 2, (half + 1) * M // 2)
                engine.tensor_tensor(
                    xh.rearrange("p (m t) -> p m t", t=PACK)[:, cols, :],
                    cosines[:, cols, :],
                    amp_home_t[:, b, :].unsqueeze(1).to_broadcast([P, M // 2, PACK]),
                    ALU.mult,
                )

        x_tiles = {}

        def legs_of_group_0():
            x = hand.tile([P, 2 * PACK * M], BF16, name="x_wide", align_bytes=64, offset=WIDE_AT[2])
            out_rows[0] = hand.tile([P, PACK, M], BF16, name="out_rows0", align_bytes=64, offset=WIDE_AT[1] + INSIDE)
            for t in range(PACK):
                nc.gpsimd.tensor_scalar(
                    out_rows[0][:, t, :], sines[0][:, t, :], amp_out_t[:, 0, t : t + 1], 0.0, ALU.mult, ALU.add
                )
            for half in range(2):
                cols = slice(half * M // 2, (half + 1) * M // 2)
                gpsimd_move(
                    x[:, : PACK * M].rearrange("p (m t) -> p m t", t=PACK)[:, cols],
                    out_rows[0][:].rearrange("p t m -> p m t")[:, cols],
                )
            home_leg(0, x[:, PACK * M :], nc.gpsimd)
            x_tiles[0] = [x[:]]

        def legs_of_group_1():
            xo = hand.tile([P, PACK * M], BF16, name="xo1", align_bytes=64, offset=WIDE_AT[2] + INSIDE)
            xh = hand.tile([P, PACK * M], BF16, name="xh1", align_bytes=64, offset=SIN1_AT + 4 * KIB)
            nc.vector.tensor_tensor(
                xo[:].rearrange("p (c i t) -> p c t i", i=4, t=PACK),
                sines[1][:].rearrange("p t (c i) -> p c t i", i=4),
                amp_out_t[:, 1, :].unsqueeze(1).unsqueeze(3).to_broadcast([P, M // 4, PACK, 4]),
                ALU.mult,
            )
            home_leg(1, xh[:], nc.gpsimd)
            x_tiles[1] = [xo[:], xh[:]]

        def quantise_legs(b):
            codes = held.tile([P, 2 * M], U32, name="x_codes", tag=f"after{X_AFTER_GATHERS[b]}", align_bytes=64)
            planes = ring.tile([P, 2 * M], U8, name="x_planes", align_bytes=64)
            width = 2 * M // len(x_tiles[b])
            for i, x in enumerate(x_tiles[b]):
                cols = slice(i * width, (i + 1) * width)
                nc.vector.quantize_mx(out=codes[:, cols].bitcast(FP8X4), scales=planes[:, cols], in_=x)
            second_passes(b, y_out, codes[:, :M], planes[:, :M])
            second_passes(b, y_home, codes[:, M:], planes[:, M:])

        def legs_of_last_group():
            xo = ring.tile([P, PACK * M], BF16, name="xo", tag="x_last", align_bytes=64)
            nc.vector.tensor_copy(
                xo[:].rearrange("p (c i t) -> p c t i", i=4, t=PACK),
                out_rows[LAST][:].rearrange("p t (c i) -> p c t i", i=4),
            )
            codes = ring.tile([P, M], U32, name="xo_codes", tag="last_codes", align_bytes=64)
            planes = ring.tile([P, M], U8, name="xo_planes", tag="last_planes", align_bytes=64)
            nc.vector.quantize_mx(out=codes[:].bitcast(FP8X4), scales=planes[:], in_=xo[:])
            second_passes(LAST, y_out, codes[:], planes[:])

            xh = ring.tile([P, PACK * M], BF16, name="xh", tag="x_last", align_bytes=64)
            home_leg(LAST, xh[:], nc.vector)
            codes = ring.tile([P, M], U32, name="xh_codes", tag="last_codes", align_bytes=64)
            planes = ring.tile([P, M], U8, name="xh_planes", tag="last_planes", align_bytes=64)
            for first in range(0, M, M // 2):
                cols = slice(first, first + M // 2)
                nc.vector.quantize_mx(
                    out=codes[:, cols].bitcast(FP8X4),
                    scales=planes[:, cols],
                    in_=xh[:, PACK * first : PACK * (first + M // 2)],
                )
                for c in range(OUT_TILES):
                    for m0 in range(first, first + M // 2, P):
                        part = slice(m0, m0 + P)
                        second_pass(LAST, c, y_home[c][:, part], codes[:, part], planes[:, part], m0 + P == M)

        legs = [legs_of_group_0, legs_of_group_1, legs_of_last_group]

        for step in range(ROW_TILES + ANGLE_LAG):
            if step < ROW_TILES:
                first_product(step)
                b, t = divmod(step, PACK)
                if t == 0 and b < LAST:
                    load_w1(b + 1)
                    weave_w1_group(b + 1)
            if step == ROW_TILES:
                for half in range(2):
                    y_home.append(psum.tile([P, M], F32, name="y_home", tag=f"z{half}", bufs=2))
                for b, c, codes, planes in owed:
                    second_pass(b, c, y_home[c][:], codes, planes, False)
            if 1 <= step <= ROW_TILES:
                gathers(step - 1)
                for b, j in W1_AFTER_GATHERS.items():
                    if j == step - 1:
                        quantise_w1_group(b)
                for b, j in X_AFTER_GATHERS.items():
                    if j == step - 1:
                        quantise_legs(b)
            if step >= ANGLE_LAG:
                angles(step - ANGLE_LAG)
                b, t = divmod(step - ANGLE_LAG, PACK)
                if t == PACK - 1:
                    legs[b]()

        for c in range(OUT_TILES):
            y_out_sb = ring.tile([P, M], F32, name="y_out_sb", bufs=OUT_TILES)
            nc.scalar.copy(y_out_sb[:], y_out[c][:])
            result = ring.tile([P, M], F32, name="result", bufs=OUT_TILES)
            nc.vector.tensor_tensor(result[:], y_home[c][:], y_out_sb[:], ALU.max)
            nc.sync.dma_start(out[c * P : (c + 1) * P, :], result[:])
